import numpy as np
import ml_dtypes


def mxq(x, axis, fmt="e4m3"):
    dtype, down = {"e4m3": (ml_dtypes.float8_e4m3fn, 7), "e5m2": (ml_dtypes.float8_e5m2, 14)}[fmt]
    v = np.moveaxis(np.asarray(x, np.float32).astype(ml_dtypes.bfloat16).astype(np.float64), axis, -1)
    blocks = v.reshape(v.shape[:-1] + (-1, 32))
    amax = np.abs(blocks).max(-1, keepdims=True)
    byte = np.maximum(np.where(amax > 0, np.frexp(amax)[1] - 1 + 127, 0) - down, 1)
    scale = np.exp2(byte - 127.0)
    codes = (blocks / scale).astype(np.float32).astype(dtype).astype(np.float64)
    return np.moveaxis((codes * scale).reshape(v.shape), -1, axis)


WIDE = False


def mx_kscale(k):
    if not WIDE:
        return np.ones(k)
    levels = np.array([10, -10, 5, -5, 0])
    if k % 512:
        return np.exp2(np.random.permutation(np.resize(levels, k // 32))).repeat(32)
    a = np.empty((k // 512, 16))
    for p in range(k // 512):
        a[p, :8] = np.random.permutation(np.resize(levels, 8))
        for g in range(8):
            far = levels[np.abs(levels - a[p, g]) >= 10]
            a[p, g + 8] = far[np.random.randint(len(far))]
    return np.exp2(a.ravel()).repeat(32)


def f64(x):
    return np.asarray(x).astype(np.float64)


def striped(idx):
    return np.tile(idx.reshape(-1, 16).T, (8, 1)).astype(np.uint16)


def unstriped(offs):
    return offs[:16].T.reshape(-1).astype(np.int64)


def pack_weight(w):
    k, n = w.shape
    w = f64(np.asarray(w, np.float32).astype(ml_dtypes.bfloat16)).reshape(k // 32, 32, n)
    amax = np.abs(w).max(1)
    byte = np.clip(np.where(amax > 0, np.frexp(amax)[1] - 1 + 127 - 7, 1), 1, 254)
    scaled = (w * np.exp2(127.0 - byte)[:, None, :]).reshape(k, n).astype(np.float32)
    words = np.ascontiguousarray(scaled.reshape(k // 512, 128, 4, n).transpose(0, 1, 3, 2)).astype(ml_dtypes.float8_e4m3fn).view(np.uint8)
    return words, np.ascontiguousarray(byte.astype(np.uint8).reshape(k // 512, 16, n))


def unpack_weight(words, scales):
    g, p, n, _ = words.shape
    vals = np.ascontiguousarray(words).view(ml_dtypes.float8_e4m3fn).astype(np.float64) * np.repeat(np.exp2(scales.astype(np.float64) - 127.0), 8, axis=1)[..., None]
    return vals.transpose(0, 1, 3, 2).reshape(g * 512, n)


def relu(v):
    return np.maximum(v, 0.0)


K, T, S, V = 512, 2048, 512, 512
P = 2 ** 7


def setup_inputs():
    n = np.random.standard_normal
    s = mx_kscale(K)[:, None]
    packed_xT = pack_weight(n((K, T)) * s)
    return {
        "x_words": packed_xT[0],
        "x_scales": packed_xT[1],
        "hT": (n((K, V)) / np.sqrt(K) / s).astype(np.float32),
        "proj": (0.6 * n((V, S))).astype(np.float32),
        "dres": (np.random.uniform(0.4, 2.0, (V, S))).astype(np.float32),
        "qual": (np.tile(np.random.uniform(0.5, 1.5, T), (P, 1))).astype(np.float32),
        "inv": (np.random.uniform(0.3, 0.7, (V, 1))).astype(np.float32),
        "offs": striped(np.random.permutation(T)[:S]),
    }


def reference(x_words, x_scales, hT, proj, dres, qual, inv, offs):
    hTq = mxq(f64(hT), 0, "e4m3")
    xq = unpack_weight(x_words, x_scales)[:, unstriped(offs)]
    y = hTq.T @ xq
    ee = f64(inv) * ((f64(qual)[:1][:, unstriped(offs)]) * y - f64(proj))
    dnew = relu(f64(dres) - ((ee) ** 2)) + 0.02
    return np.log(dnew)

@@ -1,0 +1,229 @@
+from contextlib import ExitStack
+
+import concourse.mybir as mybir
+from concourse.masks import make_identity
+
+F32 = mybir.dt.float32
+BF16 = mybir.dt.bfloat16
+I32 = mybir.dt.int32
+U32 = mybir.dt.uint32
+U16 = mybir.dt.uint16
+U8 = mybir.dt.uint8
+FP8X4 = mybir.dt.float8_e4m3fn_x4
+ALU = mybir.AluOpType
+ACT = mybir.ActivationFunctionType
+
+P = 128
+PACK = 4
+K, T, S, V = 512, 2048, 512, 512
+TILES = V // P
+HALF = S // 2
+FLOOR = 0.02
+
+FLOPS = 2 * K * S * V
+BYTES = K * T + 16 * T + 4 * (K * V + 3 * V * S + T + V) + 2 * P * (S // 16)
+
+CLAMP_ON_SCALAR = (0, 1, 2)
+
+
+def tile_picked_ydppg_log_p_kernel(
+    tc, x_words, x_scales, hT, proj, dres, qual, inv, offs, out
+):
+    nc = tc.nc
+    with ExitStack() as ctx:
+        keep = ctx.enter_context(tc.tile_pool(name="keep", bufs=1))
+        early = ctx.enter_context(tc.tile_pool(name="early", bufs=1))
+        psum = ctx.enter_context(tc.psum_pool(name="psum", bufs=1))
+
+        offsets = keep.tile([P, S // 16], U16, name="offsets")
+        nc.sync.dma_start(offsets[:], offs)
+
+        scale_table = early.tile([P, T], U8, name="scale_table", align_bytes=64, offset=4 * T)
+        qual_table = early.tile([P, T], F32, name="qual_table", align_bytes=64, offset=5 * T)
+        inv_rows = keep.tile([P, P], F32, name="inv_rows")
+        one = keep.tile([P, 8], F32, name="one")
+        warm = keep.tile([P, 8], F32, name="warm")
+        nc.vector.memset(scale_table[:].bitcast(I32), 0)
+        nc.sync.dma_start(qual_table[P - 1 : P, :], qual[0:1, :])
+        nc.vector.memset(one[:], 1.0)
+        nc.scalar.activation(warm[:], one[:], ACT.Ln)
+        nc.vector.memset(qual_table[0 : P - 1, :], 0.0)
+        nc.vector.memset(inv_rows[0 : P - TILES, :], 0.0)
+        identity = keep.tile([P, P], F32, name="identity")
+        make_identity(nc, identity[:])
+
+        h_view = hT.rearrange("(p j) t -> p j t", j=PACK)
+        h_raw = [keep.tile([P, PACK, P], F32, name=f"h_raw{n}") for n in range(TILES)]
+        h_src = [h[:] for h in h_raw]
+        word_table = early.tile([P, T], I32, name="word_table", align_bytes=64, offset=0)
+        proj_sb = [keep.tile([P, S], F32, name=f"proj{i}") for i in range(TILES)]
+        dres_sb = [keep.tile([P, S], F32, name=f"dres{i}") for i in range(TILES)]
+
+        def load_rows(dst, src, i):
+            nc.sync.dma_start(dst[i][:], src[i * P : (i + 1) * P, :])
+
+        nc.sync.dma_start(h_raw[0][:], h_view[:, :, 0:P])
+        for q in range(4):
+            nc.sync.dma_start(
+                scale_table[32 * q : 32 * q + 4, :].bitcast(I32),
+                x_scales[0, 4 * q : 4 * q + 4, :].bitcast(I32),
+            )
+        nc.sync.dma_start(word_table[:], x_words[0].rearrange("p c r -> p (c r)").bitcast(I32))
+        nc.sync.dma_start(inv_rows[P - TILES : P, :], inv.rearrange("(i p) o -> i (p o)", p=P))
+        nc.sync.dma_start(h_raw[1][:], h_view[:, :, P : 2 * P])
+        load_rows(proj_sb, proj, 0)
+        nc.sync.dma_start(h_raw[2][:], h_view[:, :, 2 * P : 3 * P])
+        nc.sync.dma_start(h_raw[3][:], h_view[:, :, 3 * P : 4 * P])
+        load_rows(dres_sb, dres, 0)
+        for i in range(1, TILES):
+            load_rows(proj_sb, proj, i)
+            load_rows(dres_sb, dres, i)
+
+        qual_row = keep.tile([P, S], F32, name="qual_row")
+        nc.vector.tensor_copy(qual_row[:], qual_table[:].indirect(offsets[:]))
+        x_planes = keep.tile([P, S], U8, name="x_planes", align_bytes=64)
+        nc.vector.tensor_copy(x_planes[:], scale_table[:].indirect(offsets[:]))
+
+        turned = psum.tile([P, S // P, P], F32, name="turned")
+        for c in range(S // P):
+            nc.tensor.transpose(turned[:, c, :], qual_row[:, c * P : (c + 1) * P], identity[:])
+        qual_col = keep.tile([P, S // P], F32, name="qual_col")
+        nc.scalar.copy(qual_col[:], turned[:, :, P - 1])
+        spread = psum.tile([P, S], F32, name="spread")
+        for c in range(S // P):
+            nc.tensor.transpose(
+                spread[:, c * P : (c + 1) * P], qual_col[:, c : c + 1].to_broadcast([P, P]), identity[:]
+            )
+        qual_all = keep.tile([P, S], F32, name="qual_all")
+        nc.scalar.copy(qual_all[:], spread[:])
+
+        inv_turned = psum.tile([P, P], F32, name="inv_turned")
+        nc.tensor.transpose(inv_turned[:], inv_rows[:], identity[:])
+        inv_col = keep.tile([P, TILES], F32, name="inv_col")
+        nc.scalar.copy(inv_col[:], inv_turned[:, P - TILES : P])
+
+        h_codes = [keep.tile([P, P], U32, name="h_codes0", align_bytes=64)] + [
+            early.tile([P, P], U32, name=f"h_codes{i}", align_bytes=64, offset=4 * P * i) for i in range(1, TILES)
+        ]
+        h_planes = [keep.tile([P, P], U8, name=f"h_planes{i}", align_bytes=64) for i in range(TILES)]
+        h_bf16 = [keep.tile([P, P * PACK], BF16, name=f"h_bf16{i}", align_bytes=64) for i in range(TILES)]
+
+        def cast(i):
+            nc.scalar.copy(
+                h_bf16[i][:].rearrange("p (c n j) -> p c j n", n=4, j=PACK),
+                h_src[i].rearrange("p j (c n) -> p c j n", n=4),
+            )
+
+        def quantize(i):
+            nc.vector.quantize_mx(out=h_codes[i][:].bitcast(FP8X4), scales=h_planes[i][:], in_=h_bf16[i][:])
+
+        x_codes = early.tile([P, S], U32, name="x_codes", align_bytes=64, offset=5 * T - 2 * S)
+
+        def gather_words(u):
+            nc.vector.tensor_copy(
+                x_codes[:, u * HALF : (u + 1) * HALF],
+                word_table[:].bitcast(U32).indirect(offsets[:, u * HALF // 16 : (u + 1) * HALF // 16]),
+            )
+
+        chunks = [(0, 0, HALF), (0, HALF, HALF), (1, 0, S), (2, 0, S), (3, 0, HALF), (3, HALF, HALF)]
+        y = {}
+        stage = {}
+
+        def product(i, c0, w):
+            bank = psum.tile([P, w], F32, name=f"y{i}_{c0}")
+            nc.tensor.matmul_mx(
+                out=bank[:],
+                lhsT=h_codes[i][:].bitcast(FP8X4),
+                lhsT_scale=h_planes[i][:],
+                rhs=x_codes[:, c0 : c0 + w].bitcast(FP8X4),
+                rhs_scale=x_planes[:, c0 : c0 + w],
+                start=True,
+                stop=True,
+            )
+            return bank
+
+        def fresh(kind, n):
+            stage[kind, n] = keep.tile([P, chunks[n][2]], F32, name=f"{kind}{n}")
+            return stage[kind, n][:]
+
+        def weigh(n):
+            i, c0, w = chunks[n]
+            nc.vector.tensor_tensor(fresh("a", n), y[n], qual_all[:, c0 : c0 + w], ALU.mult)
+
+        def take_off(n):
+            i, c0, w = chunks[n]
+            nc.vector.tensor_tensor(fresh("b", n), stage["a", n][:], proj_sb[i][:, c0 : c0 + w], ALU.subtract)
+
+        def square(n):
+            i, c0, w = chunks[n]
+            nc.scalar.activation(fresh("c", n), stage["b", n][:], ACT.Square, scale=inv_col[:, i : i + 1])
+
+        def lessen(n):
+            i, c0, w = chunks[n]
+            nc.vector.tensor_tensor(fresh("d", n), dres_sb[i][:, c0 : c0 + w], stage["c", n][:], ALU.subtract)
+
+        def clamp(n):
+            i, c0, w = chunks[n]
+            if i in CLAMP_ON_SCALAR:
+                nc.scalar.activation(fresh("e", n), stage["d", n][:], ACT.Relu)
+            else:
+                nc.vector.tensor_scalar(fresh("e", n), stage["d", n][:], 0.0, FLOOR, ALU.max, ALU.add)
+
+        def finish(n):
+            i, c0, w = chunks[n]
+            floor = FLOOR if i in CLAMP_ON_SCALAR else 0.0
+            nc.scalar.activation(fresh("f", n), stage["e", n][:], ACT.Ln, bias=floor)
+            nc.sync.dma_start(out[i * P : (i + 1) * P, c0 : c0 + w], stage["f", n][:])
+
+        cast(0)
+        quantize(0)
+        gather_words(0)
+        y[0] = product(0, 0, HALF)[:]
+        gather_words(1)
+        y[1] = product(0, HALF, HALF)[:]
+        cast(1)
+        weigh(0)
+        quantize(1)
+        y[2] = product(1, 0, S)[:]
+        weigh(1)
+        take_off(0)
+        square(0)
+        take_off(1)
+        square(1)
+        cast(2)
+        quantize(2)
+        y[3] = product(2, 0, S)[:]
+        cast(3)
+        weigh(2)
+        quantize(3)
+        last = product(3, 0, S)
+        y[4], y[5] = last[:, 0:HALF], last[:, HALF:S]
+        lessen(0)
+        take_off(2)
+        square(2)
+        lessen(1)
+        weigh(3)
+        clamp(0)
+        clamp(1)
+        finish(0)
+        finish(1)
+        lessen(2)
+        take_off(3)
+        square(3)
+        weigh(4)
+        weigh(5)
+        take_off(4)
+        square(4)
+        clamp(2)
+        lessen(3)
+        take_off(5)
+        square(5)
+        finish(2)
+        clamp(3)
+        lessen(4)
+        finish(3)
+        lessen(5)
+        clamp(4)
+        finish(4)
+        clamp(5)
+        finish(5)

@@ -23,7 +23,7 @@ FLOOR = 0.02
 FLOPS = 2 * K * S * V
 BYTES = K * T + 16 * T + 4 * (K * V + 3 * V * S + T + V) + 2 * P * (S // 16)
 
-CLAMP_ON_SCALAR = (0, 1, 2)
+CLAMP_ON_SCALAR = (0, 1)
 
 
 def tile_picked_ydppg_log_p_kernel(
@@ -45,10 +45,10 @@ def tile_picked_ydppg_log_p_kernel(
         warm = keep.tile([P, 8], F32, name="warm")
         nc.vector.memset(scale_table[:].bitcast(I32), 0)
         nc.sync.dma_start(qual_table[P - 1 : P, :], qual[0:1, :])
-        nc.vector.memset(one[:], 1.0)
+        nc.gpsimd.memset(one[:], 1.0)
         nc.scalar.activation(warm[:], one[:], ACT.Ln)
         nc.vector.memset(qual_table[0 : P - 1, :], 0.0)
-        nc.vector.memset(inv_rows[0 : P - TILES, :], 0.0)
+        nc.gpsimd.memset(inv_rows[0 : P - TILES, :], 0.0)
         identity = keep.tile([P, P], F32, name="identity")
         make_identity(nc, identity[:])
 
@@ -69,44 +69,62 @@ def tile_picked_ydppg_log_p_kernel(
                 x_scales[0, 4 * q : 4 * q + 4, :].bitcast(I32),
             )
         nc.sync.dma_start(word_table[:], x_words[0].rearrange("p c r -> p (c r)").bitcast(I32))
-        nc.sync.dma_start(inv_rows[P - TILES : P, :], inv.rearrange("(i p) o -> i (p o)", p=P))
-        nc.sync.dma_start(h_raw[1][:], h_view[:, :, P : 2 * P])
+        nc.gpsimd.dma_start(inv_rows[P - TILES : P, :], inv.rearrange("(i p) o -> i (p o)", p=P))
+        def load_h(i):
+            nc.sync.dma_start(h_raw[i][:], h_view[:, :, i * P : (i + 1) * P])
+
+        load_h(1)
         load_rows(proj_sb, proj, 0)
-        nc.sync.dma_start(h_raw[2][:], h_view[:, :, 2 * P : 3 * P])
-        nc.sync.dma_start(h_raw[3][:], h_view[:, :, 3 * P : 4 * P])
-        load_rows(dres_sb, dres, 0)
-        for i in range(1, TILES):
-            load_rows(proj_sb, proj, i)
+        load_h(2)
+        load_rows(proj_sb, proj, 1)
+        load_h(3)
+        for i in range(TILES):
             load_rows(dres_sb, dres, i)
+            if i + 2 < TILES:
+                load_rows(proj_sb, proj, i + 2)
 
         qual_row = keep.tile([P, S], F32, name="qual_row")
-        nc.vector.tensor_copy(qual_row[:], qual_table[:].indirect(offsets[:]))
+        for u in range(2):
+            nc.vector.tensor_copy(
+                qual_row[:, u * HALF : (u + 1) * HALF],
+                qual_table[:].indirect(offsets[:, u * HALF // 16 : (u + 1) * HALF // 16]),
+            )
         x_planes = keep.tile([P, S], U8, name="x_planes", align_bytes=64)
         nc.vector.tensor_copy(x_planes[:], scale_table[:].indirect(offsets[:]))
 
-        turned = psum.tile([P, S // P, P], F32, name="turned")
-        for c in range(S // P):
-            nc.tensor.transpose(turned[:, c, :], qual_row[:, c * P : (c + 1) * P], identity[:])
+        turned = [psum.tile([P, 3, P], F32, name=f"turned{u}") for u in range(2)]
+        spread = [psum.tile([P, HALF], F32, name=f"spread{u}") for u in range(2)]
         qual_col = keep.tile([P, S // P], F32, name="qual_col")
-        nc.scalar.copy(qual_col[:], turned[:, :, P - 1])
-        spread = psum.tile([P, S], F32, name="spread")
-        for c in range(S // P):
-            nc.tensor.transpose(
-                spread[:, c * P : (c + 1) * P], qual_col[:, c : c + 1].to_broadcast([P, P]), identity[:]
-            )
         qual_all = keep.tile([P, S], F32, name="qual_all")
-        nc.scalar.copy(qual_all[:], spread[:])
+        for u in range(2):
+            for c in range(2):
+                nc.tensor.transpose(
+                    turned[u][:, c, :], qual_row[:, (2 * u + c) * P : (2 * u + c + 1) * P], identity[:]
+                )
+            nc.scalar.copy(qual_col[:, 2 * u : 2 * u + 2], turned[u][:, 0:2, P - 1])
+        for u in range(2):
+            for c in range(2):
+                nc.tensor.transpose(
+                    spread[u][:, c * P : (c + 1) * P],
+                    qual_col[:, 2 * u + c : 2 * u + c + 1].to_broadcast([P, P]),
+                    identity[:],
+                )
+            nc.scalar.copy(qual_all[:, u * HALF : (u + 1) * HALF], spread[u][:])
 
-        inv_turned = psum.tile([P, P], F32, name="inv_turned")
-        nc.tensor.transpose(inv_turned[:], inv_rows[:], identity[:])
         inv_col = keep.tile([P, TILES], F32, name="inv_col")
-        nc.scalar.copy(inv_col[:], inv_turned[:, P - TILES : P])
+
+        def turn_inv():
+            nc.tensor.transpose(turned[0][:, 2, :], inv_rows[:], identity[:])
+            nc.scalar.copy(inv_col[:], turned[0][:, 2, P - TILES : P])
 
         h_codes = [keep.tile([P, P], U32, name="h_codes0", align_bytes=64)] + [
             early.tile([P, P], U32, name=f"h_codes{i}", align_bytes=64, offset=4 * P * i) for i in range(1, TILES)
         ]
         h_planes = [keep.tile([P, P], U8, name=f"h_planes{i}", align_bytes=64) for i in range(TILES)]
-        h_bf16 = [keep.tile([P, P * PACK], BF16, name=f"h_bf16{i}", align_bytes=64) for i in range(TILES)]
+        h_bf16 = [
+            early.tile([P, P * PACK], BF16, name=f"h_bf16{i}", align_bytes=64, offset=9 * T + 4 * S * i)
+            for i in range(TILES)
+        ]
 
         def cast(i):
             nc.scalar.copy(
@@ -117,113 +135,103 @@ def tile_picked_ydppg_log_p_kernel(
         def quantize(i):
             nc.vector.quantize_mx(out=h_codes[i][:].bitcast(FP8X4), scales=h_planes[i][:], in_=h_bf16[i][:])
 
-        x_codes = early.tile([P, S], U32, name="x_codes", align_bytes=64, offset=5 * T - 2 * S)
+        x_codes = [
+            early.tile([P, HALF], U32, name=f"x_codes{u}", align_bytes=64, offset=5 * T - S + 4 * HALF * u)
+            for u in range(2)
+        ]
 
         def gather_words(u):
             nc.vector.tensor_copy(
-                x_codes[:, u * HALF : (u + 1) * HALF],
+                x_codes[u][:],
                 word_table[:].bitcast(U32).indirect(offsets[:, u * HALF // 16 : (u + 1) * HALF // 16]),
             )
 
-        chunks = [(0, 0, HALF), (0, HALF, HALF), (1, 0, S), (2, 0, S), (3, 0, HALF), (3, HALF, HALF)]
-        y = {}
-        stage = {}
-
-        def product(i, c0, w):
-            bank = psum.tile([P, w], F32, name=f"y{i}_{c0}")
+        def product(i, u, bank):
             nc.tensor.matmul_mx(
-                out=bank[:],
+                out=bank,
                 lhsT=h_codes[i][:].bitcast(FP8X4),
                 lhsT_scale=h_planes[i][:],
-                rhs=x_codes[:, c0 : c0 + w].bitcast(FP8X4),
-                rhs_scale=x_planes[:, c0 : c0 + w],
+                rhs=x_codes[u][:].bitcast(FP8X4),
+                rhs_scale=x_planes[:, u * HALF : (u + 1) * HALF],
                 start=True,
                 stop=True,
             )
-            return bank
 
-        def fresh(kind, n):
-            stage[kind, n] = keep.tile([P, chunks[n][2]], F32, name=f"{kind}{n}")
-            return stage[kind, n][:]
+        y = {}
 
-        def weigh(n):
-            i, c0, w = chunks[n]
-            nc.vector.tensor_tensor(fresh("a", n), y[n], qual_all[:, c0 : c0 + w], ALU.mult)
+        def products(i, tag):
+            y[i] = psum.tile([P, S], F32, name=f"y{i}", tag=tag)
+            for u in range(2):
+                product(i, u, y[i][:, u * HALF : (u + 1) * HALF])
 
-        def take_off(n):
-            i, c0, w = chunks[n]
-            nc.vector.tensor_tensor(fresh("b", n), stage["a", n][:], proj_sb[i][:, c0 : c0 + w], ALU.subtract)
+        def stage(kind):
+            return [keep.tile([P, S], F32, name=f"{kind}{i}") for i in range(TILES)]
 
-        def square(n):
-            i, c0, w = chunks[n]
-            nc.scalar.activation(fresh("c", n), stage["b", n][:], ACT.Square, scale=inv_col[:, i : i + 1])
+        weighed, left, squared, lessened, clamped, gains = [stage(kind) for kind in "abcdef"]
+        weighed[0] = early.tile([P, S], F32, name="a_first", align_bytes=64, offset=9 * T + 4 * S)
+        whole, low, high = slice(0, S), slice(0, HALF), slice(HALF, S)
 
-        def lessen(n):
-            i, c0, w = chunks[n]
-            nc.vector.tensor_tensor(fresh("d", n), dres_sb[i][:, c0 : c0 + w], stage["c", n][:], ALU.subtract)
+        def weigh(i, cols, bank=None):
+            src = y[i][:, cols] if bank is None else bank
+            nc.vector.tensor_tensor(weighed[i][:, cols], src, qual_all[:, cols], ALU.mult)
 
-        def clamp(n):
-            i, c0, w = chunks[n]
+        def take_off(i, cols):
+            nc.vector.tensor_tensor(left[i][:, cols], weighed[i][:, cols], proj_sb[i][:, cols], ALU.subtract)
+            nc.scalar.activation(squared[i][:, cols], left[i][:, cols], ACT.Square, scale=inv_col[:, i : i + 1])
+
+        def lessen(i, cols):
+            nc.vector.tensor_tensor(lessened[i][:, cols], dres_sb[i][:, cols], squared[i][:, cols], ALU.subtract)
+
+        def clamp(i, cols):
             if i in CLAMP_ON_SCALAR:
-                nc.scalar.activation(fresh("e", n), stage["d", n][:], ACT.Relu)
+                nc.scalar.activation(clamped[i][:, cols], lessened[i][:, cols], ACT.Relu)
             else:
-                nc.vector.tensor_scalar(fresh("e", n), stage["d", n][:], 0.0, FLOOR, ALU.max, ALU.add)
+                nc.vector.tensor_scalar(clamped[i][:, cols], lessened[i][:, cols], 0.0, FLOOR, ALU.max, ALU.add)
 
-        def finish(n):
-            i, c0, w = chunks[n]
+        def finish(i, cols):
             floor = FLOOR if i in CLAMP_ON_SCALAR else 0.0
-            nc.scalar.activation(fresh("f", n), stage["e", n][:], ACT.Ln, bias=floor)
-            nc.sync.dma_start(out[i * P : (i + 1) * P, c0 : c0 + w], stage["f", n][:])
+            nc.scalar.activation(gains[i][:, cols], clamped[i][:, cols], ACT.Ln, bias=floor)
+            nc.sync.dma_start(out[i * P : (i + 1) * P, cols], gains[i][:, cols])
 
         cast(0)
         quantize(0)
-        gather_words(0)
-        y[0] = product(0, 0, HALF)[:]
-        gather_words(1)
-        y[1] = product(0, HALF, HALF)[:]
+        first = [psum.tile([P, HALF], F32, name=f"y_first{u}") for u in range(2)]
+        for u in range(2):
+            gather_words(u)
+            product(0, u, first[u][:])
+        turn_inv()
         cast(1)
-        weigh(0)
         quantize(1)
-        y[2] = product(1, 0, S)[:]
-        weigh(1)
-        take_off(0)
-        square(0)
-        take_off(1)
-        square(1)
+        products(1, "y1")
+        weigh(0, low, first[0][:])
+        weigh(0, high, first[1][:])
+        take_off(0, low)
+        take_off(0, high)
         cast(2)
+        weigh(1, whole)
         quantize(2)
-        y[3] = product(2, 0, S)[:]
+        products(2, "y2")
         cast(3)
-        weigh(2)
+        take_off(1, whole)
+        lessen(0, whole)
+        weigh(2, whole)
         quantize(3)
-        last = product(3, 0, S)
-        y[4], y[5] = last[:, 0:HALF], last[:, HALF:S]
-        lessen(0)
-        take_off(2)
-        square(2)
-        lessen(1)
-        weigh(3)
-        clamp(0)
-        clamp(1)
-        finish(0)
-        finish(1)
-        lessen(2)
-        take_off(3)
-        square(3)
-        weigh(4)
-        weigh(5)
-        take_off(4)
-        square(4)
-        clamp(2)
-        lessen(3)
-        take_off(5)
-        square(5)
-        finish(2)
-        clamp(3)
-        lessen(4)
-        finish(3)
-        lessen(5)
-        clamp(4)
-        finish(4)
-        clamp(5)
-        finish(5)
+        products(3, "turned1")
+        clamp(0, whole)
+        lessen(1, whole)
+        finish(0, whole)
+        take_off(2, whole)
+        clamp(1, whole)
+        weigh(3, whole)
+        finish(1, whole)
+        take_off(3, low)
+        take_off(3, high)
+        lessen(2, whole)
+        lessen(3, low)
+        clamp(2, whole)
+        finish(2, whole)
+        lessen(3, high)
+        clamp(3, low)
+        finish(3, low)
+        clamp(3, high)
+        finish(3, high)

@@ -35,26 +35,26 @@ def tile_picked_ydppg_log_p_kernel(
         early = ctx.enter_context(tc.tile_pool(name="early", bufs=1))
         psum = ctx.enter_context(tc.psum_pool(name="psum", bufs=1))
 
+        h_view = hT.rearrange("(p j) t -> p j t", j=PACK)
+        h_raw = [keep.tile([P, PACK, w], F32, name=f"h_raw{n}") for n, w in enumerate((P, P, 2 * P))]
+        h_src = [h_raw[0][:], h_raw[1][:], h_raw[2][:, :, 0:P], h_raw[2][:, :, P : 2 * P]]
         offsets = keep.tile([P, S // 16], U16, name="offsets")
         nc.sync.dma_start(offsets[:], offs)
 
         scale_table = early.tile([P, T], U8, name="scale_table", align_bytes=64, offset=4 * T)
         qual_table = early.tile([P, T], F32, name="qual_table", align_bytes=64, offset=5 * T)
         inv_rows = keep.tile([P, P], F32, name="inv_rows")
-        one = keep.tile([P, 8], F32, name="one")
-        warm = keep.tile([P, 8], F32, name="warm")
         nc.vector.memset(scale_table[:].bitcast(I32), 0)
         nc.sync.dma_start(qual_table[P - 1 : P, :], qual[0:1, :])
-        nc.gpsimd.memset(one[:], 1.0)
-        nc.scalar.activation(warm[:], one[:], ACT.Ln)
-        nc.vector.memset(qual_table[0 : P - 1, :], 0.0)
-        nc.gpsimd.memset(inv_rows[0 : P - TILES, :], 0.0)
+        nc.sync.dma_start(h_raw[0][:], h_view[:, :, 0:P])
         identity = keep.tile([P, P], F32, name="identity")
-        make_identity(nc, identity[:])
+        nc.vector.memset(identity[:], 0.0)
+        nc.vector.memset(qual_table[0 : P - 1, :], 0.0)
+        nc.vector.memset(inv_rows[0 : P - TILES, :], 0.0)
+        make_identity(nc, identity[:], nomemset=True)
+        warm = keep.tile([P, 8], F32, name="warm")
+        nc.scalar.activation(warm[0:64, :], inv_rows[0:64, 0:8], ACT.Ln, bias=1.0)
 
-        h_view = hT.rearrange("(p j) t -> p j t", j=PACK)
-        h_raw = [keep.tile([P, PACK, P], F32, name=f"h_raw{n}") for n in range(TILES)]
-        h_src = [h[:] for h in h_raw]
         word_table = early.tile([P, T], I32, name="word_table", align_bytes=64, offset=0)
         proj_sb = [keep.tile([P, S], F32, name=f"proj{i}") for i in range(TILES)]
         dres_sb = [keep.tile([P, S], F32, name=f"dres{i}") for i in range(TILES)]
@@ -62,22 +62,17 @@ def tile_picked_ydppg_log_p_kernel(
         def load_rows(dst, src, i):
             nc.sync.dma_start(dst[i][:], src[i * P : (i + 1) * P, :])
 
-        nc.sync.dma_start(h_raw[0][:], h_view[:, :, 0:P])
         for q in range(4):
             nc.sync.dma_start(
-                scale_table[32 * q : 32 * q + 4, :].bitcast(I32),
-                x_scales[0, 4 * q : 4 * q + 4, :].bitcast(I32),
+                scale_table[q:P:32, :].bitcast(I32),
+                x_scales[0, q:16:4, :].bitcast(I32),
             )
         nc.sync.dma_start(word_table[:], x_words[0].rearrange("p c r -> p (c r)").bitcast(I32))
-        nc.gpsimd.dma_start(inv_rows[P - TILES : P, :], inv.rearrange("(i p) o -> i (p o)", p=P))
-        def load_h(i):
-            nc.sync.dma_start(h_raw[i][:], h_view[:, :, i * P : (i + 1) * P])
-
-        load_h(1)
+        nc.sync.dma_start(h_raw[1][:], h_view[:, :, P : 2 * P])
         load_rows(proj_sb, proj, 0)
-        load_h(2)
+        nc.sync.dma_start(inv_rows[P - TILES : P, :], inv.rearrange("(i p) o -> i (p o)", p=P))
+        nc.sync.dma_start(h_raw[2][:], h_view[:, :, 2 * P : 4 * P])
         load_rows(proj_sb, proj, 1)
-        load_h(3)
         for i in range(TILES):
             load_rows(dres_sb, dres, i)
             if i + 2 < TILES:
@@ -199,10 +194,10 @@ def tile_picked_ydppg_log_p_kernel(
         for u in range(2):
             gather_words(u)
             product(0, u, first[u][:])
-        turn_inv()
         cast(1)
         quantize(1)
         products(1, "y1")
+        turn_inv()
         weigh(0, low, first[0][:])
         weigh(0, high, first[1][:])
         take_off(0, low)
@@ -232,6 +227,6 @@ def tile_picked_ydppg_log_p_kernel(
         finish(2, whole)
         lessen(3, high)
         clamp(3, low)
-        finish(3, low)
         clamp(3, high)
+        finish(3, low)
         finish(3, high)

from contextlib import ExitStack

import concourse.mybir as mybir
from concourse.masks import make_identity

F32 = mybir.dt.float32
BF16 = mybir.dt.bfloat16
I32 = mybir.dt.int32
U32 = mybir.dt.uint32
U16 = mybir.dt.uint16
U8 = mybir.dt.uint8
FP8X4 = mybir.dt.float8_e4m3fn_x4
ALU = mybir.AluOpType
ACT = mybir.ActivationFunctionType

P = 128
PACK = 4
K, T, S, V = 512, 2048, 512, 512
TILES = V // P
HALF = S // 2
FLOOR = 0.02

FLOPS = 2 * K * S * V
BYTES = K * T + 16 * T + 4 * (K * V + 3 * V * S + T + V) + 2 * P * (S // 16)

CLAMP_ON_SCALAR = (0, 1)


def tile_picked_ydppg_log_p_kernel(
    tc, x_words, x_scales, hT, proj, dres, qual, inv, offs, out
):
    nc = tc.nc
    with ExitStack() as ctx:
        keep = ctx.enter_context(tc.tile_pool(name="keep", bufs=1))
        early = ctx.enter_context(tc.tile_pool(name="early", bufs=1))
        psum = ctx.enter_context(tc.psum_pool(name="psum", bufs=1))

        h_view = hT.rearrange("(p j) t -> p j t", j=PACK)
        h_raw = [keep.tile([P, PACK, w], F32, name=f"h_raw{n}") for n, w in enumerate((P, P, 2 * P))]
        h_src = [h_raw[0][:], h_raw[1][:], h_raw[2][:, :, 0:P], h_raw[2][:, :, P : 2 * P]]
        offsets = keep.tile([P, S // 16], U16, name="offsets")
        nc.sync.dma_start(offsets[:], offs)

        scale_table = early.tile([P, T], U8, name="scale_table", align_bytes=64, offset=4 * T)
        qual_table = early.tile([P, T], F32, name="qual_table", align_bytes=64, offset=5 * T)
        inv_rows = keep.tile([P, P], F32, name="inv_rows")
        nc.vector.memset(scale_table[:].bitcast(I32), 0)
        nc.sync.dma_start(qual_table[P - 1 : P, :], qual[0:1, :])
        nc.sync.dma_start(h_raw[0][:], h_view[:, :, 0:P])
        identity = keep.tile([P, P], F32, name="identity")
        nc.vector.memset(identity[:], 0.0)
        nc.vector.memset(qual_table[0 : P - 1, :], 0.0)
        nc.vector.memset(inv_rows[0 : P - TILES, :], 0.0)
        make_identity(nc, identity[:], nomemset=True)
        warm = keep.tile([P, 8], F32, name="warm")
        nc.scalar.activation(warm[0:64, :], inv_rows[0:64, 0:8], ACT.Ln, bias=1.0)

        word_table = early.tile([P, T], I32, name="word_table", align_bytes=64, offset=0)
        proj_sb = [keep.tile([P, S], F32, name=f"proj{i}") for i in range(TILES)]
        dres_sb = [keep.tile([P, S], F32, name=f"dres{i}") for i in range(TILES)]

        def load_rows(dst, src, i):
            nc.sync.dma_start(dst[i][:], src[i * P : (i + 1) * P, :])

        for q in range(4):
            nc.sync.dma_start(
                scale_table[q:P:32, :].bitcast(I32),
                x_scales[0, q:16:4, :].bitcast(I32),
            )
        nc.sync.dma_start(word_table[:], x_words[0].rearrange("p c r -> p (c r)").bitcast(I32))
        nc.sync.dma_start(h_raw[1][:], h_view[:, :, P : 2 * P])
        load_rows(proj_sb, proj, 0)
        nc.sync.dma_start(inv_rows[P - TILES : P, :], inv.rearrange("(i p) o -> i (p o)", p=P))
        nc.sync.dma_start(h_raw[2][:], h_view[:, :, 2 * P : 4 * P])
        load_rows(proj_sb, proj, 1)
        for i in range(TILES):
            load_rows(dres_sb, dres, i)
            if i + 2 < TILES:
                load_rows(proj_sb, proj, i + 2)

        qual_row = keep.tile([P, S], F32, name="qual_row")
        for u in range(2):
            nc.vector.tensor_copy(
                qual_row[:, u * HALF : (u + 1) * HALF],
                qual_table[:].indirect(offsets[:, u * HALF // 16 : (u + 1) * HALF // 16]),
            )
        x_planes = keep.tile([P, S], U8, name="x_planes", align_bytes=64)
        nc.vector.tensor_copy(x_planes[:], scale_table[:].indirect(offsets[:]))

        turned = [psum.tile([P, 3, P], F32, name=f"turned{u}") for u in range(2)]
        spread = [psum.tile([P, HALF], F32, name=f"spread{u}") for u in range(2)]
        qual_col = keep.tile([P, S // P], F32, name="qual_col")
        qual_all = keep.tile([P, S], F32, name="qual_all")
        for u in range(2):
            for c in range(2):
                nc.tensor.transpose(
                    turned[u][:, c, :], qual_row[:, (2 * u + c) * P : (2 * u + c + 1) * P], identity[:]
                )
            nc.scalar.copy(qual_col[:, 2 * u : 2 * u + 2], turned[u][:, 0:2, P - 1])
        for u in range(2):
            for c in range(2):
                nc.tensor.transpose(
                    spread[u][:, c * P : (c + 1) * P],
                    qual_col[:, 2 * u + c : 2 * u + c + 1].to_broadcast([P, P]),
                    identity[:],
                )
            nc.scalar.copy(qual_all[:, u * HALF : (u + 1) * HALF], spread[u][:])

        inv_col = keep.tile([P, TILES], F32, name="inv_col")

        def turn_inv():
            nc.tensor.transpose(turned[0][:, 2, :], inv_rows[:], identity[:])
            nc.scalar.copy(inv_col[:], turned[0][:, 2, P - TILES : P])

        h_codes = [keep.tile([P, P], U32, name="h_codes0", align_bytes=64)] + [
            early.tile([P, P], U32, name=f"h_codes{i}", align_bytes=64, offset=4 * P * i) for i in range(1, TILES)
        ]
        h_planes = [keep.tile([P, P], U8, name=f"h_planes{i}", align_bytes=64) for i in range(TILES)]
        h_bf16 = [
            early.tile([P, P * PACK], BF16, name=f"h_bf16{i}", align_bytes=64, offset=9 * T + 4 * S * i)
            for i in range(TILES)
        ]

        def cast(i):
            nc.scalar.copy(
                h_bf16[i][:].rearrange("p (c n j) -> p c j n", n=4, j=PACK),
                h_src[i].rearrange("p j (c n) -> p c j n", n=4),
            )

        def quantize(i):
            nc.vector.quantize_mx(out=h_codes[i][:].bitcast(FP8X4), scales=h_planes[i][:], in_=h_bf16[i][:])

        x_codes = [
            early.tile([P, HALF], U32, name=f"x_codes{u}", align_bytes=64, offset=5 * T - S + 4 * HALF * u)
            for u in range(2)
        ]

        def gather_words(u):
            nc.vector.tensor_copy(
                x_codes[u][:],
                word_table[:].bitcast(U32).indirect(offsets[:, u * HALF // 16 : (u + 1) * HALF // 16]),
            )

        def product(i, u, bank):
            nc.tensor.matmul_mx(
                out=bank,
                lhsT=h_codes[i][:].bitcast(FP8X4),
                lhsT_scale=h_planes[i][:],
                rhs=x_codes[u][:].bitcast(FP8X4),
                rhs_scale=x_planes[:, u * HALF : (u + 1) * HALF],
                start=True,
                stop=True,
            )

        y = {}

        def products(i, tag):
            y[i] = psum.tile([P, S], F32, name=f"y{i}", tag=tag)
            for u in range(2):
                product(i, u, y[i][:, u * HALF : (u + 1) * HALF])

        def stage(kind):
            return [keep.tile([P, S], F32, name=f"{kind}{i}") for i in range(TILES)]

        weighed, left, squared, lessened, clamped, gains = [stage(kind) for kind in "abcdef"]
        weighed[0] = early.tile([P, S], F32, name="a_first", align_bytes=64, offset=9 * T + 4 * S)
        whole, low, high = slice(0, S), slice(0, HALF), slice(HALF, S)

        def weigh(i, cols, bank=None):
            src = y[i][:, cols] if bank is None else bank
            nc.vector.tensor_tensor(weighed[i][:, cols], src, qual_all[:, cols], ALU.mult)

        def take_off(i, cols):
            nc.vector.tensor_tensor(left[i][:, cols], weighed[i][:, cols], proj_sb[i][:, cols], ALU.subtract)
            nc.scalar.activation(squared[i][:, cols], left[i][:, cols], ACT.Square, scale=inv_col[:, i : i + 1])

        def lessen(i, cols):
            nc.vector.tensor_tensor(lessened[i][:, cols], dres_sb[i][:, cols], squared[i][:, cols], ALU.subtract)

        def clamp(i, cols):
            if i in CLAMP_ON_SCALAR:
                nc.scalar.activation(clamped[i][:, cols], lessened[i][:, cols], ACT.Relu)
            else:
                nc.vector.tensor_scalar(clamped[i][:, cols], lessened[i][:, cols], 0.0, FLOOR, ALU.max, ALU.add)

        def finish(i, cols):
            floor = FLOOR if i in CLAMP_ON_SCALAR else 0.0
            nc.scalar.activation(gains[i][:, cols], clamped[i][:, cols], ACT.Ln, bias=floor)
            nc.sync.dma_start(out[i * P : (i + 1) * P, cols], gains[i][:, cols])

        cast(0)
        quantize(0)
        first = [psum.tile([P, HALF], F32, name=f"y_first{u}") for u in range(2)]
        for u in range(2):
            gather_words(u)
            product(0, u, first[u][:])
        cast(1)
        quantize(1)
        products(1, "y1")
        turn_inv()
        weigh(0, low, first[0][:])
        weigh(0, high, first[1][:])
        take_off(0, low)
        take_off(0, high)
        cast(2)
        weigh(1, whole)
        quantize(2)
        products(2, "y2")
        cast(3)
        take_off(1, whole)
        lessen(0, whole)
        weigh(2, whole)
        quantize(3)
        products(3, "turned1")
        clamp(0, whole)
        lessen(1, whole)
        finish(0, whole)
        take_off(2, whole)
        clamp(1, whole)
        weigh(3, whole)
        finish(1, whole)
        take_off(3, low)
        take_off(3, high)
        lessen(2, whole)
        lessen(3, low)
        clamp(2, whole)
        finish(2, whole)
        lessen(3, high)
        clamp(3, low)
        clamp(3, high)
        finish(3, low)
        finish(3, high)
